import numpy as np
import ml_dtypes


def mxq(x, axis, fmt="e4m3"):
    dtype, down = {"e4m3": (ml_dtypes.float8_e4m3fn, 7), "e5m2": (ml_dtypes.float8_e5m2, 14)}[fmt]
    v = np.moveaxis(np.asarray(x, np.float32).astype(ml_dtypes.bfloat16).astype(np.float64), axis, -1)
    blocks = v.reshape(v.shape[:-1] + (-1, 32))
    amax = np.abs(blocks).max(-1, keepdims=True)
    byte = np.maximum(np.where(amax > 0, np.frexp(amax)[1] - 1 + 127, 0) - down, 1)
    scale = np.exp2(byte - 127.0)
    codes = (blocks / scale).astype(np.float32).astype(dtype).astype(np.float64)
    return np.moveaxis((codes * scale).reshape(v.shape), -1, axis)


WIDE = False


def mx_kscale(k):
    if not WIDE:
        return np.ones(k)
    levels = np.array([10, -10, 5, -5, 0])
    if k % 512:
        return np.exp2(np.random.permutation(np.resize(levels, k // 32))).repeat(32)
    a = np.empty((k // 512, 16))
    for p in range(k // 512):
        a[p, :8] = np.random.permutation(np.resize(levels, 8))
        for g in range(8):
            far = levels[np.abs(levels - a[p, g]) >= 10]
            a[p, g + 8] = far[np.random.randint(len(far))]
    return np.exp2(a.ravel()).repeat(32)


def f64(x):
    return np.asarray(x).astype(np.float64)


def striped(idx):
    return np.tile(idx.reshape(-1, 16).T, (8, 1)).astype(np.uint16)


def unstriped(offs):
    return offs[:16].T.reshape(-1).astype(np.int64)


def striped8(idx):
    return np.concatenate([x.reshape(-1, 16).T for x in idx]).astype(np.uint16)


def runs(offs, k):
    lists = np.stack([offs[16 * r : 16 * r + 16].T.reshape(-1) for r in range(8)]).astype(np.int64)
    return lists[np.arange(k) % 512 // 64]


def pack_weight(w):
    k, n = w.shape
    w = f64(np.asarray(w, np.float32).astype(ml_dtypes.bfloat16)).reshape(k // 32, 32, n)
    amax = np.abs(w).max(1)
    byte = np.clip(np.where(amax > 0, np.frexp(amax)[1] - 1 + 127 - 7, 1), 1, 254)
    scaled = (w * np.exp2(127.0 - byte)[:, None, :]).reshape(k, n).astype(np.float32)
    words = np.ascontiguousarray(scaled.reshape(k // 512, 128, 4, n).transpose(0, 1, 3, 2)).astype(ml_dtypes.float8_e4m3fn).view(np.uint8)
    return words, np.ascontiguousarray(byte.astype(np.uint8).reshape(k // 512, 16, n))


def unpack_weight(words, scales):
    g, p, n, _ = words.shape
    vals = np.ascontiguousarray(words).view(ml_dtypes.float8_e4m3fn).astype(np.float64) * np.repeat(np.exp2(scales.astype(np.float64) - 127.0), 8, axis=1)[..., None]
    return vals.transpose(0, 1, 3, 2).reshape(g * 512, n)


def sigmoid(v):
    return 1.0 / (1.0 + np.exp(-np.maximum(v, -700.0)))


K, T, S, N, H, W = 512, 2048, 512, 512, 512, 2048


def setup_inputs():
    n = np.random.standard_normal
    s = mx_kscale(K)[:, None]
    u = mx_kscale(S)
    packed_xT = pack_weight(n((K, T)) * s)
    return {
        "x_words": packed_xT[0],
        "x_scales": packed_xT[1],
        "wa": (n((K, H)) / np.sqrt(K) / s).astype(np.float32),
        "wb": (n((K, H)) / np.sqrt(K) / s).astype(np.float32),
        "gt": (np.random.uniform(0.5, 1.5, (S, 1)) * u[:, None]).astype(np.float32),
        "w1": (n((S, N)) / np.sqrt(S) / u[:, None]).astype(np.float32),
        "offs": striped(np.random.permutation(T)[:S]),
        "two": striped(np.random.permutation(T)[:S]),
        "n1": striped8(np.stack([np.random.permutation(H) for _ in range(8)])),
        "n2": striped8(np.stack([np.random.permutation(H) for _ in range(8)])),
        "n3": striped(np.random.randint(0, H, W)),
    }


def reference(x_words, x_scales, wa, wb, gt, w1, offs, two, n1, n2, n3):
    xq = unpack_weight(x_words, x_scales)[:, unstriped(offs)]
    y = xq.T @ mxq(f64(wa), 0, "e4m3")
    x_two = unpack_weight(x_words, x_scales)[:, unstriped(two)]
    d = x_two.T @ mxq(f64(wb), 0, "e4m3")
    z = f64(gt) * (y + (sigmoid(d[np.arange(S)[:, None], runs(n2, S)] - d)) * (y[np.arange(S)[:, None], runs(n1, S)] - y))
    h = mxq(f64(w1), 0, "e4m3").T @ mxq(z, 0, "e4m3")
    ex = np.exp(0.5 * h)
    mb = ex[:, unstriped(n3)]
    ms = mb.reshape(N, H, 4).sum(axis=2)
    return (4.0 * ex) / (ms + 0.5)

@@ -1,0 +1,193 @@
+from contextlib import ExitStack
+
+import concourse.mybir as mybir
+
+F32 = mybir.dt.float32
+BF16 = mybir.dt.bfloat16
+I32 = mybir.dt.int32
+U32 = mybir.dt.uint32
+U16 = mybir.dt.uint16
+U8 = mybir.dt.uint8
+FP8X4 = mybir.dt.float8_e4m3fn_x4
+ACT = mybir.ActivationFunctionType
+ALU = mybir.AluOpType
+
+P = 128
+PACK = 4
+T = 2048
+S = 512
+H = 512
+N = 512
+MEMBERS = 4
+HALF = H // 2
+FLOPS = 3 * 2 * 512 * 512 * 512
+
+
+def interleaved(tile_ap):
+    return tile_ap.rearrange("p (c i) t -> p c t i", i=4)
+
+
+def planes(tile_ap):
+    return tile_ap.rearrange("p t (c i) -> p c t i", i=4)
+
+
+def tile_picked_twtpullbgshare_none_p_kernel(
+    tc, x_words, x_scales, wa, wb, gt, w1, offs, two, n1, n2, n3, out
+):
+    nc = tc.nc
+    with ExitStack() as ctx:
+        lists = ctx.enter_context(tc.tile_pool(name="lists", bufs=1))
+        keep = ctx.enter_context(tc.tile_pool(name="keep", bufs=1))
+        ring = ctx.enter_context(tc.tile_pool(name="ring", bufs=2))
+        psum = ctx.enter_context(tc.psum_pool(name="psum", bufs=1))
+
+        def load_list(src, name):
+            tile = lists.tile(list(src.shape), U16, name=name)
+            nc.sync.dma_start(tile[:], src)
+            return tile
+
+        def load_weight(src, name):
+            tile = keep.tile([P, PACK, src.shape[1]], F32, name=name)
+            nc.sync.dma_start(tile[:], src.rearrange("(p t) c -> p t c", t=PACK))
+            return tile
+
+        def mx_tiles(name, width):
+            codes = keep.tile([P, width], U32, name=name + "_codes", align_bytes=64)
+            scales = keep.tile([P, width], U8, name=name + "_scales", align_bytes=64)
+            return codes, scales
+
+        def quantise(mx, grouped, cols):
+            nc.vector.quantize_mx(
+                out=mx[0][:, cols].bitcast(FP8X4),
+                scales=mx[1][:, cols],
+                in_=grouped[:, cols, :].rearrange("p c t -> p (c t)"),
+            )
+
+        def multiply(acc, stationary, rows, moving, cols):
+            nc.tensor.matmul_mx(
+                out=acc,
+                lhsT=stationary[0][:, rows].bitcast(FP8X4),
+                lhsT_scale=stationary[1][:, rows],
+                rhs=moving[0][:, cols].bitcast(FP8X4),
+                rhs_scale=moving[1][:, cols],
+                start=True,
+                stop=True,
+            )
+
+        table_scales = keep.tile([P, T], U8, name="table_scales")
+        nc.vector.memset(table_scales[:].bitcast(I32), 0)
+        wb_raw = load_weight(wb, "wb_raw")
+        table_words = keep.tile([P, T], U32, name="table_words")
+        nc.sync.dma_start(table_words[:].bitcast(I32), x_words[0].rearrange("p c t -> p (c t)").bitcast(I32))
+        for q in range(4):
+            nc.sync.dma_start(
+                table_scales[32 * q : 32 * q + 4, :].bitcast(I32), x_scales[0, 4 * q : 4 * q + 4, :].bitcast(I32)
+            )
+        two_list = load_list(two, "two_list")
+        offs_list = load_list(offs, "offs_list")
+        wa_raw = load_weight(wa, "wa_raw")
+        n2_list = load_list(n2, "n2_list")
+        n1_list = load_list(n1, "n1_list")
+        gate = keep.tile([P, PACK], F32, name="gate")
+        nc.sync.dma_start(gate[:], gt.rearrange("(p t) o -> p (t o)", t=PACK))
+        w1_raw = load_weight(w1, "w1_raw")
+        n3_list = load_list(n3, "n3_list")
+
+        def dealt(tile):
+            return tile[:].rearrange("p (t m) -> p m t", t=PACK)
+
+        x_two = mx_tiles("x_two", S)
+        x_idx = mx_tiles("x_idx", S)
+        wb_mx = mx_tiles("wb", H)
+        wa_mx = mx_tiles("wa", H)
+        w1_mx = mx_tiles("w1", N)
+        z_mx = mx_tiles("z", H)
+        halves = [slice(0, HALF), slice(HALF, H)]
+        everything = slice(0, H)
+
+        wb_grouped = keep.tile([P, H, PACK], BF16, name="wb_grouped", align_bytes=64)
+        wa_grouped = keep.tile([P, H, PACK], BF16, name="wa_grouped", align_bytes=64)
+        w1_grouped = keep.tile([P, N, PACK], BF16, name="w1_grouped", align_bytes=64)
+        z_grouped = keep.tile([P, H, PACK], BF16, name="z_grouped", align_bytes=64)
+
+        nc.vector.tensor_copy(dealt(x_two[1]), table_scales[:].indirect(two_list[:]))
+        split = 320
+        nc.vector.tensor_copy(interleaved(wb_grouped[:, :split, :]), planes(wb_raw[:, :, :split]))
+        nc.scalar.copy(interleaved(wb_grouped[:, split:, :]), planes(wb_raw[:, :, split:]))
+        quantise(wb_mx, wb_grouped, everything)
+        nc.vector.tensor_copy(dealt(x_idx[1]), table_scales[:].indirect(offs_list[:]))
+        nc.vector.tensor_copy(dealt(x_two[0]), table_words[:].indirect(two_list[:]))
+
+        d_acc = [psum.tile([P, H], F32, name=f"d_acc{t}", tag=f"bank{t}") for t in range(PACK)]
+        y_acc = [psum.tile([P, H], F32, name=f"y_acc{t}", tag=f"bank{PACK + t}") for t in range(PACK)]
+        d_rows = [keep.tile([P, H], F32, name=f"d_rows{t}") for t in range(PACK)]
+        y_rows = [keep.tile([P, H], F32, name=f"y_rows{t}") for t in range(PACK)]
+        d_far = keep.tile([P, PACK, H], F32, name="d_far")
+        y_far = keep.tile([P, PACK, H], F32, name="y_far")
+        d_gap = keep.tile([P, PACK, H], F32, name="d_gap")
+        y_gap = keep.tile([P, PACK, H], F32, name="y_gap")
+        lean = keep.tile([P, PACK, H], F32, name="lean")
+        pull = keep.tile([P, PACK, H], F32, name="pull")
+
+        def fetch(dst, window, offsets, first, count, **affine):
+            nc.scalar.activation(
+                out=dst, in_=window[:].indirect(offsets[:, first // 16 : (first + count) // 16]), func=ACT.Copy, **affine
+            )
+
+        for t in range(PACK):
+            multiply(d_acc[t][:], x_two, slice(t * P, (t + 1) * P), wb_mx, everything)
+        nc.vector.tensor_copy(dealt(x_idx[0]), table_words[:].indirect(offs_list[:]))
+        nc.vector.tensor_copy(interleaved(wa_grouped[:]), planes(wa_raw[:]))
+        quantise(wa_mx, wa_grouped, everything)
+        for t in range(PACK):
+            multiply(y_acc[t][:], x_idx, slice(t * P, (t + 1) * P), wa_mx, everything)
+
+        for t in range(PACK):
+            nc.scalar.copy(d_rows[t][:], d_acc[t][:])
+            for cols in halves:
+                fetch(d_far[:, t, cols], d_rows[t], n2_list, cols.start, HALF)
+        for t in range(PACK):
+            nc.vector.tensor_scalar(y_rows[t][:], y_acc[t][:], gate[:, t : t + 1], 0.5, ALU.mult, ALU.mult)
+        for t in range(PACK):
+            nc.vector.tensor_tensor(d_gap[:, t, :], d_acc[t][:], d_far[:, t, :], ALU.subtract)
+        nc.vector.tensor_copy(interleaved(w1_grouped[:]), planes(w1_raw[:]))
+        quantise(w1_mx, w1_grouped, everything)
+
+        h_acc = [psum.tile([P, H], F32, name=f"h_acc{r}", tag=f"bank{r}") for r in range(N // P)]
+        ex_rows = [keep.tile([P, H], F32, name=f"ex_rows{r}") for r in range(N // P)]
+
+        for cols in halves:
+            for t in range(PACK):
+                fetch(y_far[:, t, cols], y_rows[t], n1_list, cols.start, HALF, scale=2.0)
+            nc.scalar.activation(out=lean[:, :, cols], in_=d_gap[:, :, cols], func=ACT.Tanh, scale=0.5)
+            for t in range(PACK):
+                nc.vector.scalar_tensor_tensor(
+                    y_gap[:, t, cols], y_far[:, t, cols], -0.5, y_rows[t][:, cols], ALU.mult, ALU.add
+                )
+            nc.vector.scalar_tensor_tensor(pull[:, :, cols], lean[:, :, cols], 1.0, y_gap[:, :, cols], ALU.add, ALU.mult)
+            nc.vector.tensor_tensor(
+                interleaved(z_grouped[:, cols, :]), planes(pull[:, :, cols]), planes(y_far[:, :, cols]), ALU.add
+            )
+            quantise(z_mx, z_grouped, cols)
+            for r in range(N // P):
+                multiply(h_acc[r][:, cols], w1_mx, slice(r * P, (r + 1) * P), z_mx, cols)
+
+        pieces = [(0, 104), (104, 208), (208, 312), (312, 416), (416, 512)]
+        for r in range(N // P):
+            nc.scalar.activation(out=ex_rows[r][:], in_=h_acc[r][:], func=ACT.Exp, scale=0.5)
+            members = ring.tile([P, H, MEMBERS], F32, name="members")
+            pairs = ring.tile([P, H, 2], F32, name="pairs")
+            denom = ring.tile([P, H], F32, name="denom")
+            inverse = ring.tile([P, H], F32, name="inverse")
+            result = ring.tile([P, H], F32, name="result")
+            for c0, c1 in pieces:
+                fetch(
+                    members[:, c0:c1, :].rearrange("p c m -> p (c m)"), ex_rows[r], n3_list, MEMBERS * c0,
+                    MEMBERS * (c1 - c0), scale=0.25, bias=0.03125,
+                )
+            for c0, c1 in pieces:
+                nc.vector.tensor_tensor(pairs[:, c0:c1, :], members[:, c0:c1, 0:2], members[:, c0:c1, 2:4], ALU.add)
+                nc.vector.tensor_tensor(denom[:, c0:c1], pairs[:, c0:c1, 0], pairs[:, c0:c1, 1], ALU.add)
+                nc.vector.reciprocal(inverse[:, c0:c1], denom[:, c0:c1])
+                nc.vector.tensor_tensor(result[:, c0:c1], inverse[:, c0:c1], ex_rows[r][:, c0:c1], ALU.mult)
+            nc.sync.dma_start(out[r * P : (r + 1) * P, :], result[:])

@@ -1,3 +1,4 @@
+import math
 from contextlib import ExitStack
 
 import concourse.mybir as mybir
@@ -20,6 +21,7 @@ H = 512
 N = 512
 MEMBERS = 4
 HALF = H // 2
+SHIFT = -41.0
 FLOPS = 3 * 2 * 512 * 512 * 512
 
 
@@ -47,7 +49,7 @@ def tile_picked_twtpullbgshare_none_p_kernel(
             return tile
 
         def load_weight(src, name):
-            tile = keep.tile([P, PACK, src.shape[1]], F32, name=name)
+            tile = keep.tile([P, PACK, src.shape[1]], F32, name=name, align_bytes=64)
             nc.sync.dma_start(tile[:], src.rearrange("(p t) c -> p t c", t=PACK))
             return tile
 
@@ -76,28 +78,29 @@ def tile_picked_twtpullbgshare_none_p_kernel(
 
         table_scales = keep.tile([P, T], U8, name="table_scales")
         nc.vector.memset(table_scales[:].bitcast(I32), 0)
-        wb_raw = load_weight(wb, "wb_raw")
+        two_list = load_list(two, "two_list")
+        offs_list = load_list(offs, "offs_list")
+        n2_list = load_list(n2, "n2_list")
+        n1_list = load_list(n1, "n1_list")
+        n3_list = load_list(n3, "n3_list")
+        gate = keep.tile([P, PACK], F32, name="gate")
+        nc.sync.dma_start(gate[:], gt.rearrange("(p t) o -> p (t o)", t=PACK))
         table_words = keep.tile([P, T], U32, name="table_words")
-        nc.sync.dma_start(table_words[:].bitcast(I32), x_words[0].rearrange("p c t -> p (c t)").bitcast(I32))
+        words_in = x_words[0].rearrange("p c t -> p (c t)").bitcast(I32)
+        for c0 in (0, T // 2):
+            nc.sync.dma_start(table_words[:].bitcast(I32)[:, c0 : c0 + T // 2], words_in[:, c0 : c0 + T // 2])
         for q in range(4):
             nc.sync.dma_start(
                 table_scales[32 * q : 32 * q + 4, :].bitcast(I32), x_scales[0, 4 * q : 4 * q + 4, :].bitcast(I32)
             )
-        two_list = load_list(two, "two_list")
-        offs_list = load_list(offs, "offs_list")
-        wa_raw = load_weight(wa, "wa_raw")
-        n2_list = load_list(n2, "n2_list")
-        n1_list = load_list(n1, "n1_list")
-        gate = keep.tile([P, PACK], F32, name="gate")
-        nc.sync.dma_start(gate[:], gt.rearrange("(p t) o -> p (t o)", t=PACK))
+        wb_raw = [load_weight(wb[:, :HALF], "wb_raw0"), load_weight(wb[:, HALF:], "wb_raw1")]
+        wa_raw = [load_weight(wa[:, :HALF], "wa_raw0"), load_weight(wa[:, HALF:], "wa_raw1")]
         w1_raw = load_weight(w1, "w1_raw")
-        n3_list = load_list(n3, "n3_list")
 
         def dealt(tile):
             return tile[:].rearrange("p (t m) -> p m t", t=PACK)
 
         x_two = mx_tiles("x_two", S)
-        x_idx = mx_tiles("x_idx", S)
         wb_mx = mx_tiles("wb", H)
         wa_mx = mx_tiles("wa", H)
         w1_mx = mx_tiles("w1", N)
@@ -107,24 +110,12 @@ def tile_picked_twtpullbgshare_none_p_kernel(
 
         wb_grouped = keep.tile([P, H, PACK], BF16, name="wb_grouped", align_bytes=64)
         wa_grouped = keep.tile([P, H, PACK], BF16, name="wa_grouped", align_bytes=64)
-        w1_grouped = keep.tile([P, N, PACK], BF16, name="w1_grouped", align_bytes=64)
         z_grouped = keep.tile([P, H, PACK], BF16, name="z_grouped", align_bytes=64)
-
-        nc.vector.tensor_copy(dealt(x_two[1]), table_scales[:].indirect(two_list[:]))
-        split = 320
-        nc.vector.tensor_copy(interleaved(wb_grouped[:, :split, :]), planes(wb_raw[:, :, :split]))
-        nc.scalar.copy(interleaved(wb_grouped[:, split:, :]), planes(wb_raw[:, :, split:]))
-        quantise(wb_mx, wb_grouped, everything)
-        nc.vector.tensor_copy(dealt(x_idx[1]), table_scales[:].indirect(offs_list[:]))
-        nc.vector.tensor_copy(dealt(x_two[0]), table_words[:].indirect(two_list[:]))
 
         d_acc = [psum.tile([P, H], F32, name=f"d_acc{t}", tag=f"bank{t}") for t in range(PACK)]
         y_acc = [psum.tile([P, H], F32, name=f"y_acc{t}", tag=f"bank{PACK + t}") for t in range(PACK)]
         d_rows = [keep.tile([P, H], F32, name=f"d_rows{t}") for t in range(PACK)]
         y_rows = [keep.tile([P, H], F32, name=f"y_rows{t}") for t in range(PACK)]
-        d_far = keep.tile([P, PACK, H], F32, name="d_far")
-        y_far = keep.tile([P, PACK, H], F32, name="y_far")
-        d_gap = keep.tile([P, PACK, H], F32, name="d_gap")
         y_gap = keep.tile([P, PACK, H], F32, name="y_gap")
         lean = keep.tile([P, PACK, H], F32, name="lean")
         pull = keep.tile([P, PACK, H], F32, name="pull")
@@ -134,60 +125,160 @@ def tile_picked_twtpullbgshare_none_p_kernel(
                 out=dst, in_=window[:].indirect(offsets[:, first // 16 : (first + count) // 16]), func=ACT.Copy, **affine
             )
 
+        half_gate = keep.tile([P, PACK], F32, name="half_gate")
+        nc.scalar.activation(out=half_gate[:], in_=gate[:], func=ACT.Copy, scale=0.5)
+        nc.vector.tensor_copy(dealt(x_two[0]), table_words[:].indirect(two_list[:]))
+        nc.vector.tensor_copy(dealt(x_two[1]), table_scales[:].indirect(two_list[:]))
+        for half, raw in zip(halves, wb_raw):
+            nc.scalar.copy(interleaved(wb_grouped[:, half, :]), planes(raw[:]))
+        quantise(wb_mx, wb_grouped, everything)
         for t in range(PACK):
             multiply(d_acc[t][:], x_two, slice(t * P, (t + 1) * P), wb_mx, everything)
+        x_idx = (
+            keep.tile([P, S], U32, name="x_idx_codes", align_bytes=64),
+            keep.tile([P, S], U8, name="x_idx_scales", tag="wb_grouped", align_bytes=64),
+        )
         nc.vector.tensor_copy(dealt(x_idx[0]), table_words[:].indirect(offs_list[:]))
-        nc.vector.tensor_copy(interleaved(wa_grouped[:]), planes(wa_raw[:]))
+        nc.vector.tensor_copy(dealt(x_idx[1]), table_scales[:].indirect(offs_list[:]))
+        nc.scalar.copy(interleaved(wa_grouped[:, halves[0], :]), planes(wa_raw[0][:]))
+        nc.vector.tensor_copy(d_rows[2][:], d_acc[2][:])
+        nc.vector.tensor_copy(interleaved(wa_grouped[:, halves[1], :]), planes(wa_raw[1][:]))
         quantise(wa_mx, wa_grouped, everything)
+        nc.vector.tensor_copy(d_rows[3][:], d_acc[3][:])
         for t in range(PACK):
             multiply(y_acc[t][:], x_idx, slice(t * P, (t + 1) * P), wa_mx, everything)
 
-        for t in range(PACK):
-            nc.scalar.copy(d_rows[t][:], d_acc[t][:])
-            for cols in halves:
-                fetch(d_far[:, t, cols], d_rows[t], n2_list, cols.start, HALF)
-        for t in range(PACK):
-            nc.vector.tensor_scalar(y_rows[t][:], y_acc[t][:], gate[:, t : t + 1], 0.5, ALU.mult, ALU.mult)
-        for t in range(PACK):
-            nc.vector.tensor_tensor(d_gap[:, t, :], d_acc[t][:], d_far[:, t, :], ALU.subtract)
-        nc.vector.tensor_copy(interleaved(w1_grouped[:]), planes(w1_raw[:]))
-        quantise(w1_mx, w1_grouped, everything)
-
-        h_acc = [psum.tile([P, H], F32, name=f"h_acc{r}", tag=f"bank{r}") for r in range(N // P)]
-        ex_rows = [keep.tile([P, H], F32, name=f"ex_rows{r}") for r in range(N // P)]
-
-        for cols in halves:
+        def fetch_d(cols):
+            d_far = keep.tile([P, PACK, HALF], F32, name="d_far")
             for t in range(PACK):
-                fetch(y_far[:, t, cols], y_rows[t], n1_list, cols.start, HALF, scale=2.0)
-            nc.scalar.activation(out=lean[:, :, cols], in_=d_gap[:, :, cols], func=ACT.Tanh, scale=0.5)
+                if cols.start == 0 and t < 2:
+                    nc.scalar.copy(d_rows[t][:], d_acc[t][:])
+                fetch(d_far[:, t, :], d_rows[t], n2_list, cols.start, HALF)
+            return d_far
+
+        def gap_d(cols, d_far, tag):
+            d_gap = keep.tile([P, PACK, HALF], F32, name="d_gap", tag=tag, align_bytes=64)
+            for t in range(PACK):
+                nc.vector.tensor_tensor(d_gap[:, t, :], d_acc[t][:, cols], d_far[:, t, :], ALU.subtract)
+            return d_gap
+
+        def fetch_y(cols, tag, d_gap=None):
+            y_far = keep.tile([P, PACK, cols.stop - cols.start], F32, name="y_far", tag=tag, align_bytes=64)
+            for t in range(PACK):
+                fetch(y_far[:, t, :], y_rows[t], n1_list, cols.start, cols.stop - cols.start, scale=2.0)
+                if t == 1 and d_gap is not None:
+                    nc.scalar.activation(out=lean[:, :, cols], in_=d_gap[:], func=ACT.Tanh, scale=0.5)
+            return y_far
+
+        def blend(cols, y_far):
             for t in range(PACK):
                 nc.vector.scalar_tensor_tensor(
-                    y_gap[:, t, cols], y_far[:, t, cols], -0.5, y_rows[t][:, cols], ALU.mult, ALU.add
+                    y_gap[:, t, cols], y_far[:, t, :], -0.5, y_rows[t][:, cols], ALU.mult, ALU.add
                 )
-            nc.vector.scalar_tensor_tensor(pull[:, :, cols], lean[:, :, cols], 1.0, y_gap[:, :, cols], ALU.add, ALU.mult)
-            nc.vector.tensor_tensor(
-                interleaved(z_grouped[:, cols, :]), planes(pull[:, :, cols]), planes(y_far[:, :, cols]), ALU.add
-            )
+                if t % 2 == 1:
+                    ts = slice(t - 1, t + 1)
+                    nc.vector.scalar_tensor_tensor(
+                        pull[:, ts, cols], lean[:, ts, cols], 1.0, y_gap[:, ts, cols], ALU.add, ALU.mult
+                    )
+            nc.vector.tensor_tensor(interleaved(z_grouped[:, cols, :]), planes(pull[:, :, cols]), planes(y_far[:]), ALU.add)
             quantise(z_mx, z_grouped, cols)
-            for r in range(N // P):
-                multiply(h_acc[r][:, cols], w1_mx, slice(r * P, (r + 1) * P), z_mx, cols)
 
-        pieces = [(0, 104), (104, 208), (208, 312), (312, 416), (416, 512)]
+        first, third, fourth = slice(0, 256), slice(256, 384), slice(384, 512)
+        d_far = fetch_d(halves[0])
+        for t in range(PACK):
+            nc.vector.tensor_scalar(y_rows[t][:], y_acc[t][:], half_gate[:, t : t + 1], None, ALU.mult)
+            if t == 1:
+                d_gap = gap_d(halves[0], d_far, "wa_raw1")
+        w1_grouped = keep.tile([P, N, PACK], BF16, name="w1_grouped", tag="wa_grouped", align_bytes=64)
+        nc.gpsimd.tensor_scalar(w1_grouped[:], w1_raw[:].rearrange("p t c -> p c t"), 1.0, 0.0, ALU.mult, ALU.add)
+        quantise(w1_mx, w1_grouped, everything)
+        y_far = fetch_y(first, "y_far_first", d_gap)
+        blend(first, y_far)
+        d_far = fetch_d(halves[1])
+        d_gap = gap_d(halves[1], d_far, "d_gap_second")
+        y_far = fetch_y(third, "wa_raw1")
+        nc.scalar.activation(out=lean[:, :, halves[1]], in_=d_gap[:], func=ACT.Tanh, scale=0.5)
+        blend(third, y_far)
+        y_far = fetch_y(fourth, "d_gap_second")
+        blend(fourth, y_far)
+
+        ex_rows = [keep.tile([P, H], F32, name=f"ex_rows{r}", tag=f"y_rows{r}") for r in range(N // P)]
+
+        shift = keep.tile([P, 1], F32, name="shift")
+        nc.gpsimd.memset(shift[:], SHIFT)
+
+        def mix(cols, accs):
+            for r in range(N // P):
+                multiply(accs[r], w1_mx, slice(r * P, (r + 1) * P), z_mx, cols)
+            for r in range(N // P):
+                nc.scalar.activation(out=ex_rows[r][:, cols], in_=accs[r], func=ACT.Exp, scale=0.5, bias=shift[:])
+
+        h_first = [psum.tile([P, 2, HALF], F32, name=f"h_first{b}", tag=f"bank{PACK + b}") for b in range(2)]
+        mix(first, [h_first[r // 2][:, r % 2, :] for r in range(N // P)])
+        h_third = psum.tile([P, N // P, 128], F32, name="h_third", tag=f"bank{PACK + 2}")
+        mix(third, [h_third[:, r, :] for r in range(N // P)])
+        h_fourth = [psum.tile([P, 128], F32, name=f"h_fourth{r}", tag=f"bank{r}") for r in range(N // P)]
+        mix(fourth, [h_fourth[r][:] for r in range(N // P)])
+
+        steps = []
         for r in range(N // P):
-            nc.scalar.activation(out=ex_rows[r][:], in_=h_acc[r][:], func=ACT.Exp, scale=0.5)
+            edges = (0, 64, 176, 288, 400, 512) if r == 0 else (0, 112, 224, 336, 448, 512)
             members = ring.tile([P, H, MEMBERS], F32, name="members")
             pairs = ring.tile([P, H, 2], F32, name="pairs")
             denom = ring.tile([P, H], F32, name="denom")
+            product = ring.tile([P, HALF], F32, name="product")
+            shared = ring.tile([P, HALF], F32, name="shared")
             inverse = ring.tile([P, H], F32, name="inverse")
             result = ring.tile([P, H], F32, name="result")
-            for c0, c1 in pieces:
-                fetch(
-                    members[:, c0:c1, :].rearrange("p c m -> p (c m)"), ex_rows[r], n3_list, MEMBERS * c0,
-                    MEMBERS * (c1 - c0), scale=0.25, bias=0.03125,
-                )
-            for c0, c1 in pieces:
-                nc.vector.tensor_tensor(pairs[:, c0:c1, :], members[:, c0:c1, 0:2], members[:, c0:c1, 2:4], ALU.add)
-                nc.vector.tensor_tensor(denom[:, c0:c1], pairs[:, c0:c1, 0], pairs[:, c0:c1, 1], ALU.add)
-                nc.vector.reciprocal(inverse[:, c0:c1], denom[:, c0:c1])
-                nc.vector.tensor_tensor(result[:, c0:c1], inverse[:, c0:c1], ex_rows[r][:, c0:c1], ALU.mult)
-            nc.sync.dma_start(out[r * P : (r + 1) * P, :], result[:])
+            for c0, c1 in zip(edges, edges[1:]):
+                steps.append((r, c0, c1, members, pairs, denom, product, shared, inverse, result))
+
+        def gather_members(r, c0, c1, members, pairs, denom, product, shared, inverse, result):
+            fetch(
+                members[:, c0:c1, :].rearrange("p c m -> p (c m)"), ex_rows[r], n3_list, MEMBERS * c0,
+                MEMBERS * (c1 - c0), scale=0.25, bias=0.03125 * math.exp(SHIFT),
+            )
+            nc.vector.tensor_tensor(pairs[:, c0:c1, :], members[:, c0:c1, 0:2], members[:, c0:c1, 2:4], ALU.add)
+
+        def add_pairs(r, c0, c1, members, pairs, denom, product, shared, inverse, result):
+            nc.vector.tensor_tensor(denom[:, c0:c1], pairs[:, c0:c1, 0], pairs[:, c0:c1, 1], ALU.add)
+
+        def multiply_halves(r, c0, c1, members, pairs, denom, product, shared, inverse, result):
+            mid = (c0 + c1) // 2
+            nc.vector.tensor_tensor(product[:, c0 // 2 : c1 // 2], denom[:, c0:mid], denom[:, mid:c1], ALU.mult)
+
+        def finish(r, c0, c1, members, pairs, denom, product, shared, inverse, result):
+            last = r == N // P - 1
+            nc.vector.reciprocal(shared[:, c0 // 2 : c1 // 2], product[:, c0 // 2 : c1 // 2])
+            if last:
+                group_start = {224: 0, 336: 224, 448: 336, 512: 448}
+            elif r == 0:
+                group_start = {64: 0, 288: 64, 512: 288}
+            else:
+                group_start = {224: 0, 448: 224, 512: 448}
+            if c1 not in group_start:
+                return
+            g0 = group_start[c1]
+            half = (c1 - c0) // 2
+            engine = nc.vector if last and c1 > 336 else nc.gpsimd
+            mates = denom[:, g0:c1].rearrange("p (s h c) -> p s h c", h=2, c=half)
+            inverses = inverse[:, g0:c1].rearrange("p (s h c) -> p s h c", h=2, c=half)
+            common = shared[:, g0 // 2 : c1 // 2].rearrange("p (s c) -> p s c", c=half)
+            for h in range(2):
+                engine.tensor_tensor(inverses[:, :, h, :], common, mates[:, :, 1 - h, :], ALU.mult)
+            engine.tensor_tensor(result[:, g0:c1], inverse[:, g0:c1], ex_rows[r][:, g0:c1], ALU.mult)
+            if last and c1 in (336, 512):
+                stored = 0 if c1 == 336 else 336
+                nc.sync.dma_start(out[r * P : (r + 1) * P, stored:c1], result[:, stored:c1])
+            elif c1 == H:
+                nc.sync.dma_start(out[r * P : (r + 1) * P, :], result[:])
+
+        for now, before in zip(steps + [None], [None] + steps):
+            if now is not None:
+                gather_members(*now)
+            if before is not None:
+                multiply_halves(*before)
+            if now is not None:
+                add_pairs(*now)
+            if before is not None:
+                finish(*before)

@@ -22,6 +22,14 @@ N = 512
 MEMBERS = 4
 HALF = H // 2
 SHIFT = -41.0
+MATE = 8
+GROUPS = [
+    [(64,), (112,), (112,), (112,), (112,)],
+    [(112,), (112,), (112,), (112, 64)],
+    [(88, 88), (88, 88), (80, 80)],
+    [(96, 96), (112,), (96,), (64,), (48,)],
+]
+SCALE_AT = [(288, 512), (224, 512), (352, 512), (192, 304, 512)]
 FLOPS = 3 * 2 * 512 * 512 * 512
 
 
@@ -220,65 +228,51 @@ def tile_picked_twtpullbgshare_none_p_kernel(
         h_fourth = [psum.tile([P, 128], F32, name=f"h_fourth{r}", tag=f"bank{r}") for r in range(N // P)]
         mix(fourth, [h_fourth[r][:] for r in range(N // P)])
 
-        steps = []
-        for r in range(N // P):
-            edges = (0, 64, 176, 288, 400, 512) if r == 0 else (0, 112, 224, 336, 448, 512)
+        tiles = N // P
+
+        def mates(ap):
+            return ap.rearrange("p (s h c) -> p s h c", h=2, c=MATE)
+
+        def invert(r, work, c0, c1, engine):
+            denom, product, shared, inverse, result = work
+            both = slice(c0 // 2, c1 // 2)
+            nc.vector.tensor_reduce(
+                product[:, both].rearrange("p (s c) -> p s c", c=MATE),
+                denom[:, c0:c1].rearrange("p (s h c) -> p s c h", h=2, c=MATE),
+                mybir.AxisListType.X,
+                ALU.mult,
+            )
+            nc.vector.reciprocal(shared[:, both], product[:, both])
+
+        def scale(r, work, c0, c1, engine):
+            denom, product, shared, inverse, result = work
+            common = shared[:, c0 // 2 : c1 // 2].rearrange("p (s c) -> p s c", c=MATE)
+            for h in range(2):
+                engine.tensor_tensor(
+                    mates(inverse[:, c0:c1])[:, :, h, :], common, mates(denom[:, c0:c1])[:, :, 1 - h, :], ALU.mult
+                )
+            engine.tensor_tensor(result[:, c0:c1], inverse[:, c0:c1], ex_rows[r][:, c0:c1], ALU.mult)
+            nc.sync.dma_start(out[r * P : (r + 1) * P, c0:c1], result[:, c0:c1])
+
+        for r in range(tiles):
             members = ring.tile([P, H, MEMBERS], F32, name="members")
-            pairs = ring.tile([P, H, 2], F32, name="pairs")
             denom = ring.tile([P, H], F32, name="denom")
             product = ring.tile([P, HALF], F32, name="product")
             shared = ring.tile([P, HALF], F32, name="shared")
             inverse = ring.tile([P, H], F32, name="inverse")
             result = ring.tile([P, H], F32, name="result")
-            for c0, c1 in zip(edges, edges[1:]):
-                steps.append((r, c0, c1, members, pairs, denom, product, shared, inverse, result))
-
-        def gather_members(r, c0, c1, members, pairs, denom, product, shared, inverse, result):
-            fetch(
-                members[:, c0:c1, :].rearrange("p c m -> p (c m)"), ex_rows[r], n3_list, MEMBERS * c0,
-                MEMBERS * (c1 - c0), scale=0.25, bias=0.03125 * math.exp(SHIFT),
-            )
-            nc.vector.tensor_tensor(pairs[:, c0:c1, :], members[:, c0:c1, 0:2], members[:, c0:c1, 2:4], ALU.add)
-
-        def add_pairs(r, c0, c1, members, pairs, denom, product, shared, inverse, result):
-            nc.vector.tensor_tensor(denom[:, c0:c1], pairs[:, c0:c1, 0], pairs[:, c0:c1, 1], ALU.add)
-
-        def multiply_halves(r, c0, c1, members, pairs, denom, product, shared, inverse, result):
-            mid = (c0 + c1) // 2
-            nc.vector.tensor_tensor(product[:, c0 // 2 : c1 // 2], denom[:, c0:mid], denom[:, mid:c1], ALU.mult)
-
-        def finish(r, c0, c1, members, pairs, denom, product, shared, inverse, result):
-            last = r == N // P - 1
-            nc.vector.reciprocal(shared[:, c0 // 2 : c1 // 2], product[:, c0 // 2 : c1 // 2])
-            if last:
-                group_start = {224: 0, 336: 224, 448: 336, 512: 448}
-            elif r == 0:
-                group_start = {64: 0, 288: 64, 512: 288}
-            else:
-                group_start = {224: 0, 448: 224, 512: 448}
-            if c1 not in group_start:
-                return
-            g0 = group_start[c1]
-            half = (c1 - c0) // 2
-            engine = nc.vector if last and c1 > 336 else nc.gpsimd
-            mates = denom[:, g0:c1].rearrange("p (s h c) -> p s h c", h=2, c=half)
-            inverses = inverse[:, g0:c1].rearrange("p (s h c) -> p s h c", h=2, c=half)
-            common = shared[:, g0 // 2 : c1 // 2].rearrange("p (s c) -> p s c", c=half)
-            for h in range(2):
-                engine.tensor_tensor(inverses[:, :, h, :], common, mates[:, :, 1 - h, :], ALU.mult)
-            engine.tensor_tensor(result[:, g0:c1], inverse[:, g0:c1], ex_rows[r][:, g0:c1], ALU.mult)
-            if last and c1 in (336, 512):
-                stored = 0 if c1 == 336 else 336
-                nc.sync.dma_start(out[r * P : (r + 1) * P, stored:c1], result[:, stored:c1])
-            elif c1 == H:
-                nc.sync.dma_start(out[r * P : (r + 1) * P, :], result[:])
-
-        for now, before in zip(steps + [None], [None] + steps):
-            if now is not None:
-                gather_members(*now)
-            if before is not None:
-                multiply_halves(*before)
-            if now is not None:
-                add_pairs(*now)
-            if before is not None:
-                finish(*before)
+            work = (denom, product, shared, inverse, result)
+            fetched = scaled = 0
+            for group in GROUPS[r]:
+                c0 = fetched
+                for width in group:
+                    fetch(
+                        members[:, fetched : fetched + width, :].rearrange("p c m -> p (c m)"), ex_rows[r], n3_list,
+                        MEMBERS * fetched, MEMBERS * width, scale=0.25, bias=0.03125 * math.exp(SHIFT),
+                    )
+                    fetched = fetched + width
+                nc.vector.tensor_reduce(denom[:, c0:fetched], members[:, c0:fetched, :], mybir.AxisListType.X, ALU.add)
+                invert(r, work, c0, fetched, None)
+                if fetched in SCALE_AT[r]:
+                    scale(r, work, scaled, fetched, nc.vector if r == tiles - 1 and fetched == H else nc.gpsimd)
+                    scaled = fetched

@@ -12,33 +12,48 @@ U8 = mybir.dt.uint8
 FP8X4 = mybir.dt.float8_e4m3fn_x4
 ACT = mybir.ActivationFunctionType
 ALU = mybir.AluOpType
+LAST_AXIS = mybir.AxisListType.X
 
 P = 128
-PACK = 4
+PLANES = 4
 T = 2048
 S = 512
 H = 512
 N = 512
 MEMBERS = 4
 HALF = H // 2
-SHIFT = -41.0
+ROW_TILES = N // P
+LIST_ROWS = 16
+RUN = 4
 MATE = 8
-GROUPS = [
-    [(64,), (112,), (112,), (112,), (112,)],
-    [(112,), (112,), (112,), (112, 64)],
-    [(88, 88), (88, 88), (80, 80)],
-    [(96, 96), (112,), (96,), (64,), (48,)],
-]
-SCALE_AT = [(288, 512), (224, 512), (352, 512), (192, 304, 512)]
+SHIFT = -41.0
+WIDE = 112
+NARROW = H - 4 * WIDE
 FLOPS = 3 * 2 * 512 * 512 * 512
 
 
-def interleaved(tile_ap):
-    return tile_ap.rearrange("p (c i) t -> p c t i", i=4)
+def interleaved(grouped):
+    return grouped.rearrange("p (c i) t -> p c t i", i=RUN)
 
 
-def planes(tile_ap):
-    return tile_ap.rearrange("p t (c i) -> p c t i", i=4)
+def by_planes(raw):
+    return raw.rearrange("p t (c i) -> p c t i", i=RUN)
+
+
+def dealt(tile):
+    return tile[:].rearrange("p (t m) -> p m t", t=PLANES)
+
+
+def mates(columns):
+    return columns.rearrange("p (s h c) -> p s h c", h=2, c=MATE)
+
+
+def member_groups(r):
+    if r == 0:
+        return [(NARROW,)] + [(WIDE,)] * 4
+    if r == ROW_TILES - 1:
+        return [(WIDE,)] * 4 + [(NARROW,)]
+    return [(WIDE,)] * 3 + [(WIDE, NARROW)]
 
 
 def tile_picked_twtpullbgshare_none_p_kernel(
@@ -50,6 +65,8 @@ def tile_picked_twtpullbgshare_none_p_kernel(
         keep = ctx.enter_context(tc.tile_pool(name="keep", bufs=1))
         ring = ctx.enter_context(tc.tile_pool(name="ring", bufs=2))
         psum = ctx.enter_context(tc.psum_pool(name="psum", bufs=1))
+        halves = [slice(0, HALF), slice(HALF, H)]
+        everything = slice(0, H)
 
         def load_list(src, name):
             tile = lists.tile(list(src.shape), U16, name=name)
@@ -57,8 +74,8 @@ def tile_picked_twtpullbgshare_none_p_kernel(
             return tile
 
         def load_weight(src, name):
-            tile = keep.tile([P, PACK, src.shape[1]], F32, name=name, align_bytes=64)
-            nc.sync.dma_start(tile[:], src.rearrange("(p t) c -> p t c", t=PACK))
+            tile = keep.tile([P, PLANES, src.shape[1]], F32, name=name, align_bytes=64)
+            nc.sync.dma_start(tile[:], src.rearrange("(p t) c -> p t c", t=PLANES))
             return tile
 
         def mx_tiles(name, width):
@@ -73,7 +90,8 @@ def tile_picked_twtpullbgshare_none_p_kernel(
                 in_=grouped[:, cols, :].rearrange("p c t -> p (c t)"),
             )
 
-        def multiply(acc, stationary, rows, moving, cols):
+        def multiply(acc, stationary, block, moving, cols):
+            rows = slice(block * P, (block + 1) * P)
             nc.tensor.matmul_mx(
                 out=acc,
                 lhsT=stationary[0][:, rows].bitcast(FP8X4),
@@ -84,195 +102,180 @@ def tile_picked_twtpullbgshare_none_p_kernel(
                 stop=True,
             )
 
+        def fetch(dst, window, offsets, first, count, **affine):
+            entries = offsets[:, first // LIST_ROWS : (first + count) // LIST_ROWS]
+            nc.scalar.activation(out=dst, in_=window[:].indirect(entries), func=ACT.Copy, **affine)
+
         table_scales = keep.tile([P, T], U8, name="table_scales")
         nc.vector.memset(table_scales[:].bitcast(I32), 0)
+        gate = keep.tile([P, PLANES], F32, name="gate")
+        nc.gpsimd.dma_start(gate[:], gt.rearrange("(p t) o -> p (t o)", t=PLANES))
         two_list = load_list(two, "two_list")
         offs_list = load_list(offs, "offs_list")
         n2_list = load_list(n2, "n2_list")
         n1_list = load_list(n1, "n1_list")
-        n3_list = load_list(n3, "n3_list")
-        gate = keep.tile([P, PACK], F32, name="gate")
-        nc.sync.dma_start(gate[:], gt.rearrange("(p t) o -> p (t o)", t=PACK))
         table_words = keep.tile([P, T], U32, name="table_words")
         words_in = x_words[0].rearrange("p c t -> p (c t)").bitcast(I32)
         for c0 in (0, T // 2):
             nc.sync.dma_start(table_words[:].bitcast(I32)[:, c0 : c0 + T // 2], words_in[:, c0 : c0 + T // 2])
+        wb_raw = [load_weight(wb[:, halves[0]], "wb_raw0")]
+        n3_list = load_list(n3, "n3_list")
         for q in range(4):
             nc.sync.dma_start(
                 table_scales[32 * q : 32 * q + 4, :].bitcast(I32), x_scales[0, 4 * q : 4 * q + 4, :].bitcast(I32)
             )
-        wb_raw = [load_weight(wb[:, :HALF], "wb_raw0"), load_weight(wb[:, HALF:], "wb_raw1")]
-        wa_raw = [load_weight(wa[:, :HALF], "wa_raw0"), load_weight(wa[:, HALF:], "wa_raw1")]
+        wb_raw.append(load_weight(wb[:, halves[1]], "wb_raw1"))
+        wa_raw = [load_weight(wa[:, halves[0]], "wa_raw0"), load_weight(wa[:, halves[1]], "wa_raw1")]
         w1_raw = load_weight(w1, "w1_raw")
-
-        def dealt(tile):
-            return tile[:].rearrange("p (t m) -> p m t", t=PACK)
 
         x_two = mx_tiles("x_two", S)
         wb_mx = mx_tiles("wb", H)
         wa_mx = mx_tiles("wa", H)
         w1_mx = mx_tiles("w1", N)
         z_mx = mx_tiles("z", H)
-        halves = [slice(0, HALF), slice(HALF, H)]
-        everything = slice(0, H)
+        wb_grouped = keep.tile([P, H, PLANES], BF16, name="wb_grouped", align_bytes=64)
+        wa_grouped = keep.tile([P, H, PLANES], BF16, name="wa_grouped", align_bytes=64)
+        z_grouped = keep.tile([P, H, PLANES], BF16, name="z_grouped", align_bytes=64)
+        d_acc = [psum.tile([P, H], F32, name=f"d_acc{t}", tag=f"bank{t}") for t in range(PLANES)]
+        y_acc = [psum.tile([P, H], F32, name=f"y_acc{t}", tag=f"bank{PLANES + t}") for t in range(PLANES)]
+        d_rows = [keep.tile([P, H], F32, name=f"d_rows{t}") for t in range(PLANES)]
+        y_rows = [keep.tile([P, H], F32, name=f"y_rows{t}") for t in range(PLANES)]
+        y_gap = keep.tile([P, PLANES, H], F32, name="y_gap")
+        lean = keep.tile([P, PLANES, H], F32, name="lean")
+        pull = keep.tile([P, PLANES, H], F32, name="pull")
 
-        wb_grouped = keep.tile([P, H, PACK], BF16, name="wb_grouped", align_bytes=64)
-        wa_grouped = keep.tile([P, H, PACK], BF16, name="wa_grouped", align_bytes=64)
-        z_grouped = keep.tile([P, H, PACK], BF16, name="z_grouped", align_bytes=64)
-
-        d_acc = [psum.tile([P, H], F32, name=f"d_acc{t}", tag=f"bank{t}") for t in range(PACK)]
-        y_acc = [psum.tile([P, H], F32, name=f"y_acc{t}", tag=f"bank{PACK + t}") for t in range(PACK)]
-        d_rows = [keep.tile([P, H], F32, name=f"d_rows{t}") for t in range(PACK)]
-        y_rows = [keep.tile([P, H], F32, name=f"y_rows{t}") for t in range(PACK)]
-        y_gap = keep.tile([P, PACK, H], F32, name="y_gap")
-        lean = keep.tile([P, PACK, H], F32, name="lean")
-        pull = keep.tile([P, PACK, H], F32, name="pull")
-
-        def fetch(dst, window, offsets, first, count, **affine):
-            nc.scalar.activation(
-                out=dst, in_=window[:].indirect(offsets[:, first // 16 : (first + count) // 16]), func=ACT.Copy, **affine
-            )
-
-        half_gate = keep.tile([P, PACK], F32, name="half_gate")
+        half_gate = keep.tile([P, PLANES], F32, name="half_gate")
         nc.scalar.activation(out=half_gate[:], in_=gate[:], func=ACT.Copy, scale=0.5)
         nc.vector.tensor_copy(dealt(x_two[0]), table_words[:].indirect(two_list[:]))
         nc.vector.tensor_copy(dealt(x_two[1]), table_scales[:].indirect(two_list[:]))
         for half, raw in zip(halves, wb_raw):
-            nc.scalar.copy(interleaved(wb_grouped[:, half, :]), planes(raw[:]))
-        quantise(wb_mx, wb_grouped, everything)
-        for t in range(PACK):
-            multiply(d_acc[t][:], x_two, slice(t * P, (t + 1) * P), wb_mx, everything)
+            nc.scalar.copy(interleaved(wb_grouped[:, half, :]), by_planes(raw[:]))
+            quantise(wb_mx, wb_grouped, half)
+        for t in range(PLANES):
+            multiply(d_acc[t][:], x_two, t, wb_mx, everything)
         x_idx = (
             keep.tile([P, S], U32, name="x_idx_codes", align_bytes=64),
             keep.tile([P, S], U8, name="x_idx_scales", tag="wb_grouped", align_bytes=64),
         )
         nc.vector.tensor_copy(dealt(x_idx[0]), table_words[:].indirect(offs_list[:]))
         nc.vector.tensor_copy(dealt(x_idx[1]), table_scales[:].indirect(offs_list[:]))
-        nc.scalar.copy(interleaved(wa_grouped[:, halves[0], :]), planes(wa_raw[0][:]))
+        nc.scalar.copy(interleaved(wa_grouped[:, halves[0], :]), by_planes(wa_raw[0][:]))
         nc.vector.tensor_copy(d_rows[2][:], d_acc[2][:])
-        nc.vector.tensor_copy(interleaved(wa_grouped[:, halves[1], :]), planes(wa_raw[1][:]))
+        nc.vector.tensor_copy(interleaved(wa_grouped[:, halves[1], :]), by_planes(wa_raw[1][:]))
         quantise(wa_mx, wa_grouped, everything)
         nc.vector.tensor_copy(d_rows[3][:], d_acc[3][:])
-        for t in range(PACK):
-            multiply(y_acc[t][:], x_idx, slice(t * P, (t + 1) * P), wa_mx, everything)
+        for t in range(PLANES):
+            multiply(y_acc[t][:], x_idx, t, wa_mx, everything)
 
         def fetch_d(cols):
-            d_far = keep.tile([P, PACK, HALF], F32, name="d_far")
-            for t in range(PACK):
+            d_far = keep.tile([P, PLANES, HALF], F32, name="d_far")
+            for t in range(PLANES):
                 if cols.start == 0 and t < 2:
                     nc.scalar.copy(d_rows[t][:], d_acc[t][:])
                 fetch(d_far[:, t, :], d_rows[t], n2_list, cols.start, HALF)
             return d_far
 
         def gap_d(cols, d_far, tag):
-            d_gap = keep.tile([P, PACK, HALF], F32, name="d_gap", tag=tag, align_bytes=64)
-            for t in range(PACK):
+            d_gap = keep.tile([P, PLANES, HALF], F32, name="d_gap", tag=tag, align_bytes=64)
+            for t in range(PLANES):
                 nc.vector.tensor_tensor(d_gap[:, t, :], d_acc[t][:, cols], d_far[:, t, :], ALU.subtract)
             return d_gap
 
-        def fetch_y(cols, tag, d_gap=None):
-            y_far = keep.tile([P, PACK, cols.stop - cols.start], F32, name="y_far", tag=tag, align_bytes=64)
-            for t in range(PACK):
-                fetch(y_far[:, t, :], y_rows[t], n1_list, cols.start, cols.stop - cols.start, scale=2.0)
-                if t == 1 and d_gap is not None:
+        def fetch_y(cols, tag, d_gap):
+            y_far = keep.tile([P, PLANES, HALF], F32, name="y_far", tag=tag, align_bytes=64)
+            for t in range(PLANES):
+                fetch(y_far[:, t, :], y_rows[t], n1_list, cols.start, HALF, scale=2.0)
+                if t == 1:
                     nc.scalar.activation(out=lean[:, :, cols], in_=d_gap[:], func=ACT.Tanh, scale=0.5)
             return y_far
 
         def blend(cols, y_far):
-            for t in range(PACK):
+            for t in range(PLANES):
                 nc.vector.scalar_tensor_tensor(
                     y_gap[:, t, cols], y_far[:, t, :], -0.5, y_rows[t][:, cols], ALU.mult, ALU.add
                 )
                 if t % 2 == 1:
-                    ts = slice(t - 1, t + 1)
+                    pair = slice(t - 1, t + 1)
                     nc.vector.scalar_tensor_tensor(
-                        pull[:, ts, cols], lean[:, ts, cols], 1.0, y_gap[:, ts, cols], ALU.add, ALU.mult
+                        pull[:, pair, cols], lean[:, pair, cols], 1.0, y_gap[:, pair, cols], ALU.add, ALU.mult
                     )
-            nc.vector.tensor_tensor(interleaved(z_grouped[:, cols, :]), planes(pull[:, :, cols]), planes(y_far[:]), ALU.add)
+            nc.vector.tensor_tensor(
+                interleaved(z_grouped[:, cols, :]), by_planes(pull[:, :, cols]), by_planes(y_far[:]), ALU.add
+            )
             quantise(z_mx, z_grouped, cols)
 
-        first, third, fourth = slice(0, 256), slice(256, 384), slice(384, 512)
         d_far = fetch_d(halves[0])
-        for t in range(PACK):
+        for t in range(PLANES):
             nc.vector.tensor_scalar(y_rows[t][:], y_acc[t][:], half_gate[:, t : t + 1], None, ALU.mult)
             if t == 1:
                 d_gap = gap_d(halves[0], d_far, "wa_raw1")
-        w1_grouped = keep.tile([P, N, PACK], BF16, name="w1_grouped", tag="wa_grouped", align_bytes=64)
+        w1_grouped = keep.tile([P, N, PLANES], BF16, name="w1_grouped", tag="wa_grouped", align_bytes=64)
         nc.gpsimd.tensor_scalar(w1_grouped[:], w1_raw[:].rearrange("p t c -> p c t"), 1.0, 0.0, ALU.mult, ALU.add)
         quantise(w1_mx, w1_grouped, everything)
-        y_far = fetch_y(first, "y_far_first", d_gap)
-        blend(first, y_far)
+        y_far = fetch_y(halves[0], "y_far_first", d_gap)
+        blend(halves[0], y_far)
         d_far = fetch_d(halves[1])
         d_gap = gap_d(halves[1], d_far, "d_gap_second")
-        y_far = fetch_y(third, "wa_raw1")
-        nc.scalar.activation(out=lean[:, :, halves[1]], in_=d_gap[:], func=ACT.Tanh, scale=0.5)
-        blend(third, y_far)
-        y_far = fetch_y(fourth, "d_gap_second")
-        blend(fourth, y_far)
+        y_far = fetch_y(halves[1], "wa_raw1", d_gap)
+        blend(halves[1], y_far)
 
-        ex_rows = [keep.tile([P, H], F32, name=f"ex_rows{r}", tag=f"y_rows{r}") for r in range(N // P)]
-
+        ex_rows = [keep.tile([P, H], F32, name=f"ex_rows{r}", tag=f"y_rows{r}") for r in range(ROW_TILES)]
         shift = keep.tile([P, 1], F32, name="shift")
         nc.gpsimd.memset(shift[:], SHIFT)
 
         def mix(cols, accs):
-            for r in range(N // P):
-                multiply(accs[r], w1_mx, slice(r * P, (r + 1) * P), z_mx, cols)
-            for r in range(N // P):
+            for r in range(ROW_TILES):
+                multiply(accs[r], w1_mx, r, z_mx, cols)
+            for r in range(ROW_TILES):
                 nc.scalar.activation(out=ex_rows[r][:, cols], in_=accs[r], func=ACT.Exp, scale=0.5, bias=shift[:])
 
-        h_first = [psum.tile([P, 2, HALF], F32, name=f"h_first{b}", tag=f"bank{PACK + b}") for b in range(2)]
-        mix(first, [h_first[r // 2][:, r % 2, :] for r in range(N // P)])
-        h_third = psum.tile([P, N // P, 128], F32, name="h_third", tag=f"bank{PACK + 2}")
-        mix(third, [h_third[:, r, :] for r in range(N // P)])
-        h_fourth = [psum.tile([P, 128], F32, name=f"h_fourth{r}", tag=f"bank{r}") for r in range(N // P)]
-        mix(fourth, [h_fourth[r][:] for r in range(N // P)])
+        h_first = [psum.tile([P, 2, HALF], F32, name=f"h_first{b}", tag=f"bank{PLANES + b}") for b in range(2)]
+        mix(halves[0], [h_first[r // 2][:, r % 2, :] for r in range(ROW_TILES)])
+        h_second = [psum.tile([P, HALF], F32, name=f"h_second{r}", tag=f"bank{r}") for r in range(ROW_TILES)]
+        mix(halves[1], [h_second[r][:] for r in range(ROW_TILES)])
 
-        tiles = N // P
-
-        def mates(ap):
-            return ap.rearrange("p (s h c) -> p s h c", h=2, c=MATE)
-
-        def invert(r, work, c0, c1, engine):
-            denom, product, shared, inverse, result = work
-            both = slice(c0 // 2, c1 // 2)
-            nc.vector.tensor_reduce(
-                product[:, both].rearrange("p (s c) -> p s c", c=MATE),
-                denom[:, c0:c1].rearrange("p (s h c) -> p s c h", h=2, c=MATE),
-                mybir.AxisListType.X,
-                ALU.mult,
-            )
-            nc.vector.reciprocal(shared[:, both], product[:, both])
-
-        def scale(r, work, c0, c1, engine):
-            denom, product, shared, inverse, result = work
-            common = shared[:, c0 // 2 : c1 // 2].rearrange("p (s c) -> p s c", c=MATE)
-            for h in range(2):
-                engine.tensor_tensor(
-                    mates(inverse[:, c0:c1])[:, :, h, :], common, mates(denom[:, c0:c1])[:, :, 1 - h, :], ALU.mult
-                )
-            engine.tensor_tensor(result[:, c0:c1], inverse[:, c0:c1], ex_rows[r][:, c0:c1], ALU.mult)
-            nc.sync.dma_start(out[r * P : (r + 1) * P, c0:c1], result[:, c0:c1])
-
-        for r in range(tiles):
+        for r in range(ROW_TILES):
+            last = r == ROW_TILES - 1
             members = ring.tile([P, H, MEMBERS], F32, name="members")
             denom = ring.tile([P, H], F32, name="denom")
             product = ring.tile([P, HALF], F32, name="product")
             shared = ring.tile([P, HALF], F32, name="shared")
             inverse = ring.tile([P, H], F32, name="inverse")
             result = ring.tile([P, H], F32, name="result")
-            work = (denom, product, shared, inverse, result)
-            fetched = scaled = 0
-            for group in GROUPS[r]:
-                c0 = fetched
+            groups = member_groups(r)
+            scale_after = {1, 2, len(groups) - 1} if last else {1, len(groups) - 1}
+            fetched = 0
+            scaled = 0
+            for g, group in enumerate(groups):
+                start = fetched
                 for width in group:
                     fetch(
-                        members[:, fetched : fetched + width, :].rearrange("p c m -> p (c m)"), ex_rows[r], n3_list,
-                        MEMBERS * fetched, MEMBERS * width, scale=0.25, bias=0.03125 * math.exp(SHIFT),
+                        members[:, fetched : fetched + width, :].rearrange("p c m -> p (c m)"),
+                        ex_rows[r],
+                        n3_list,
+                        MEMBERS * fetched,
+                        MEMBERS * width,
+                        scale=0.25,
+                        bias=0.03125 * math.exp(SHIFT),
                     )
                     fetched = fetched + width
-                nc.vector.tensor_reduce(denom[:, c0:fetched], members[:, c0:fetched, :], mybir.AxisListType.X, ALU.add)
-                invert(r, work, c0, fetched, None)
-                if fetched in SCALE_AT[r]:
-                    scale(r, work, scaled, fetched, nc.vector if r == tiles - 1 and fetched == H else nc.gpsimd)
+                couples = slice(start // 2, fetched // 2)
+                nc.vector.tensor_reduce(denom[:, start:fetched], members[:, start:fetched, :], LAST_AXIS, ALU.add)
+                nc.vector.tensor_reduce(
+                    product[:, couples].rearrange("p (s c) -> p s c", c=MATE),
+                    denom[:, start:fetched].rearrange("p (s h c) -> p s c h", h=2, c=MATE),
+                    LAST_AXIS,
+                    ALU.mult,
+                )
+                nc.vector.reciprocal(shared[:, couples], product[:, couples])
+                if g in scale_after:
+                    cols = slice(scaled, fetched)
+                    engine = nc.vector if last and fetched == H else nc.gpsimd
+                    common = shared[:, scaled // 2 : fetched // 2].rearrange("p (s c) -> p s c", c=MATE)
+                    for h in range(2):
+                        engine.tensor_tensor(
+                            mates(inverse[:, cols])[:, :, h, :], common, mates(denom[:, cols])[:, :, 1 - h, :], ALU.mult
+                        )
+                    engine.tensor_tensor(result[:, cols], inverse[:, cols], ex_rows[r][:, cols], ALU.mult)
+                    nc.sync.dma_start(out[r * P : (r + 1) * P, cols], result[:, cols])
                     scaled = fetched

import math
from contextlib import ExitStack

import concourse.mybir as mybir

F32 = mybir.dt.float32
BF16 = mybir.dt.bfloat16
I32 = mybir.dt.int32
U32 = mybir.dt.uint32
U16 = mybir.dt.uint16
U8 = mybir.dt.uint8
FP8X4 = mybir.dt.float8_e4m3fn_x4
ACT = mybir.ActivationFunctionType
ALU = mybir.AluOpType
LAST_AXIS = mybir.AxisListType.X

P = 128
PLANES = 4
T = 2048
S = 512
H = 512
N = 512
MEMBERS = 4
HALF = H // 2
ROW_TILES = N // P
LIST_ROWS = 16
RUN = 4
MATE = 8
SHIFT = -41.0
WIDE = 112
NARROW = H - 4 * WIDE
FLOPS = 3 * 2 * 512 * 512 * 512


def interleaved(grouped):
    return grouped.rearrange("p (c i) t -> p c t i", i=RUN)


def by_planes(raw):
    return raw.rearrange("p t (c i) -> p c t i", i=RUN)


def dealt(tile):
    return tile[:].rearrange("p (t m) -> p m t", t=PLANES)


def mates(columns):
    return columns.rearrange("p (s h c) -> p s h c", h=2, c=MATE)


def member_groups(r):
    if r == 0:
        return [(NARROW,)] + [(WIDE,)] * 4
    if r == ROW_TILES - 1:
        return [(WIDE,)] * 4 + [(NARROW,)]
    return [(WIDE,)] * 3 + [(WIDE, NARROW)]


def tile_picked_twtpullbgshare_none_p_kernel(
    tc, x_words, x_scales, wa, wb, gt, w1, offs, two, n1, n2, n3, out
):
    nc = tc.nc
    with ExitStack() as ctx:
        lists = ctx.enter_context(tc.tile_pool(name="lists", bufs=1))
        keep = ctx.enter_context(tc.tile_pool(name="keep", bufs=1))
        ring = ctx.enter_context(tc.tile_pool(name="ring", bufs=2))
        psum = ctx.enter_context(tc.psum_pool(name="psum", bufs=1))
        halves = [slice(0, HALF), slice(HALF, H)]
        everything = slice(0, H)

        def load_list(src, name):
            tile = lists.tile(list(src.shape), U16, name=name)
            nc.sync.dma_start(tile[:], src)
            return tile

        def load_weight(src, name):
            tile = keep.tile([P, PLANES, src.shape[1]], F32, name=name, align_bytes=64)
            nc.sync.dma_start(tile[:], src.rearrange("(p t) c -> p t c", t=PLANES))
            return tile

        def mx_tiles(name, width):
            codes = keep.tile([P, width], U32, name=name + "_codes", align_bytes=64)
            scales = keep.tile([P, width], U8, name=name + "_scales", align_bytes=64)
            return codes, scales

        def quantise(mx, grouped, cols):
            nc.vector.quantize_mx(
                out=mx[0][:, cols].bitcast(FP8X4),
                scales=mx[1][:, cols],
                in_=grouped[:, cols, :].rearrange("p c t -> p (c t)"),
            )

        def multiply(acc, stationary, block, moving, cols):
            rows = slice(block * P, (block + 1) * P)
            nc.tensor.matmul_mx(
                out=acc,
                lhsT=stationary[0][:, rows].bitcast(FP8X4),
                lhsT_scale=stationary[1][:, rows],
                rhs=moving[0][:, cols].bitcast(FP8X4),
                rhs_scale=moving[1][:, cols],
                start=True,
                stop=True,
            )

        def fetch(dst, window, offsets, first, count, **affine):
            entries = offsets[:, first // LIST_ROWS : (first + count) // LIST_ROWS]
            nc.scalar.activation(out=dst, in_=window[:].indirect(entries), func=ACT.Copy, **affine)

        table_scales = keep.tile([P, T], U8, name="table_scales")
        nc.vector.memset(table_scales[:].bitcast(I32), 0)
        gate = keep.tile([P, PLANES], F32, name="gate")
        nc.gpsimd.dma_start(gate[:], gt.rearrange("(p t) o -> p (t o)", t=PLANES))
        two_list = load_list(two, "two_list")
        offs_list = load_list(offs, "offs_list")
        n2_list = load_list(n2, "n2_list")
        n1_list = load_list(n1, "n1_list")
        table_words = keep.tile([P, T], U32, name="table_words")
        words_in = x_words[0].rearrange("p c t -> p (c t)").bitcast(I32)
        for c0 in (0, T // 2):
            nc.sync.dma_start(table_words[:].bitcast(I32)[:, c0 : c0 + T // 2], words_in[:, c0 : c0 + T // 2])
        wb_raw = [load_weight(wb[:, halves[0]], "wb_raw0")]
        n3_list = load_list(n3, "n3_list")
        for q in range(4):
            nc.sync.dma_start(
                table_scales[32 * q : 32 * q + 4, :].bitcast(I32), x_scales[0, 4 * q : 4 * q + 4, :].bitcast(I32)
            )
        wb_raw.append(load_weight(wb[:, halves[1]], "wb_raw1"))
        wa_raw = [load_weight(wa[:, halves[0]], "wa_raw0"), load_weight(wa[:, halves[1]], "wa_raw1")]
        w1_raw = load_weight(w1, "w1_raw")

        x_two = mx_tiles("x_two", S)
        wb_mx = mx_tiles("wb", H)
        wa_mx = mx_tiles("wa", H)
        w1_mx = mx_tiles("w1", N)
        z_mx = mx_tiles("z", H)
        wb_grouped = keep.tile([P, H, PLANES], BF16, name="wb_grouped", align_bytes=64)
        wa_grouped = keep.tile([P, H, PLANES], BF16, name="wa_grouped", align_bytes=64)
        z_grouped = keep.tile([P, H, PLANES], BF16, name="z_grouped", align_bytes=64)
        d_acc = [psum.tile([P, H], F32, name=f"d_acc{t}", tag=f"bank{t}") for t in range(PLANES)]
        y_acc = [psum.tile([P, H], F32, name=f"y_acc{t}", tag=f"bank{PLANES + t}") for t in range(PLANES)]
        d_rows = [keep.tile([P, H], F32, name=f"d_rows{t}") for t in range(PLANES)]
        y_rows = [keep.tile([P, H], F32, name=f"y_rows{t}") for t in range(PLANES)]
        y_gap = keep.tile([P, PLANES, H], F32, name="y_gap")
        lean = keep.tile([P, PLANES, H], F32, name="lean")
        pull = keep.tile([P, PLANES, H], F32, name="pull")

        half_gate = keep.tile([P, PLANES], F32, name="half_gate")
        nc.scalar.activation(out=half_gate[:], in_=gate[:], func=ACT.Copy, scale=0.5)
        nc.vector.tensor_copy(dealt(x_two[0]), table_words[:].indirect(two_list[:]))
        nc.vector.tensor_copy(dealt(x_two[1]), table_scales[:].indirect(two_list[:]))
        for half, raw in zip(halves, wb_raw):
            nc.scalar.copy(interleaved(wb_grouped[:, half, :]), by_planes(raw[:]))
            quantise(wb_mx, wb_grouped, half)
        for t in range(PLANES):
            multiply(d_acc[t][:], x_two, t, wb_mx, everything)
        x_idx = (
            keep.tile([P, S], U32, name="x_idx_codes", align_bytes=64),
            keep.tile([P, S], U8, name="x_idx_scales", tag="wb_grouped", align_bytes=64),
        )
        nc.vector.tensor_copy(dealt(x_idx[0]), table_words[:].indirect(offs_list[:]))
        nc.vector.tensor_copy(dealt(x_idx[1]), table_scales[:].indirect(offs_list[:]))
        nc.scalar.copy(interleaved(wa_grouped[:, halves[0], :]), by_planes(wa_raw[0][:]))
        nc.vector.tensor_copy(d_rows[2][:], d_acc[2][:])
        nc.vector.tensor_copy(interleaved(wa_grouped[:, halves[1], :]), by_planes(wa_raw[1][:]))
        quantise(wa_mx, wa_grouped, everything)
        nc.vector.tensor_copy(d_rows[3][:], d_acc[3][:])
        for t in range(PLANES):
            multiply(y_acc[t][:], x_idx, t, wa_mx, everything)

        def fetch_d(cols):
            d_far = keep.tile([P, PLANES, HALF], F32, name="d_far")
            for t in range(PLANES):
                if cols.start == 0 and t < 2:
                    nc.scalar.copy(d_rows[t][:], d_acc[t][:])
                fetch(d_far[:, t, :], d_rows[t], n2_list, cols.start, HALF)
            return d_far

        def gap_d(cols, d_far, tag):
            d_gap = keep.tile([P, PLANES, HALF], F32, name="d_gap", tag=tag, align_bytes=64)
            for t in range(PLANES):
                nc.vector.tensor_tensor(d_gap[:, t, :], d_acc[t][:, cols], d_far[:, t, :], ALU.subtract)
            return d_gap

        def fetch_y(cols, tag, d_gap):
            y_far = keep.tile([P, PLANES, HALF], F32, name="y_far", tag=tag, align_bytes=64)
            for t in range(PLANES):
                fetch(y_far[:, t, :], y_rows[t], n1_list, cols.start, HALF, scale=2.0)
                if t == 1:
                    nc.scalar.activation(out=lean[:, :, cols], in_=d_gap[:], func=ACT.Tanh, scale=0.5)
            return y_far

        def blend(cols, y_far):
            for t in range(PLANES):
                nc.vector.scalar_tensor_tensor(
                    y_gap[:, t, cols], y_far[:, t, :], -0.5, y_rows[t][:, cols], ALU.mult, ALU.add
                )
                if t % 2 == 1:
                    pair = slice(t - 1, t + 1)
                    nc.vector.scalar_tensor_tensor(
                        pull[:, pair, cols], lean[:, pair, cols], 1.0, y_gap[:, pair, cols], ALU.add, ALU.mult
                    )
            nc.vector.tensor_tensor(
                interleaved(z_grouped[:, cols, :]), by_planes(pull[:, :, cols]), by_planes(y_far[:]), ALU.add
            )
            quantise(z_mx, z_grouped, cols)

        d_far = fetch_d(halves[0])
        for t in range(PLANES):
            nc.vector.tensor_scalar(y_rows[t][:], y_acc[t][:], half_gate[:, t : t + 1], None, ALU.mult)
            if t == 1:
                d_gap = gap_d(halves[0], d_far, "wa_raw1")
        w1_grouped = keep.tile([P, N, PLANES], BF16, name="w1_grouped", tag="wa_grouped", align_bytes=64)
        nc.gpsimd.tensor_scalar(w1_grouped[:], w1_raw[:].rearrange("p t c -> p c t"), 1.0, 0.0, ALU.mult, ALU.add)
        quantise(w1_mx, w1_grouped, everything)
        y_far = fetch_y(halves[0], "y_far_first", d_gap)
        blend(halves[0], y_far)
        d_far = fetch_d(halves[1])
        d_gap = gap_d(halves[1], d_far, "d_gap_second")
        y_far = fetch_y(halves[1], "wa_raw1", d_gap)
        blend(halves[1], y_far)

        ex_rows = [keep.tile([P, H], F32, name=f"ex_rows{r}", tag=f"y_rows{r}") for r in range(ROW_TILES)]
        shift = keep.tile([P, 1], F32, name="shift")
        nc.gpsimd.memset(shift[:], SHIFT)

        def mix(cols, accs):
            for r in range(ROW_TILES):
                multiply(accs[r], w1_mx, r, z_mx, cols)
            for r in range(ROW_TILES):
                nc.scalar.activation(out=ex_rows[r][:, cols], in_=accs[r], func=ACT.Exp, scale=0.5, bias=shift[:])

        h_first = [psum.tile([P, 2, HALF], F32, name=f"h_first{b}", tag=f"bank{PLANES + b}") for b in range(2)]
        mix(halves[0], [h_first[r // 2][:, r % 2, :] for r in range(ROW_TILES)])
        h_second = [psum.tile([P, HALF], F32, name=f"h_second{r}", tag=f"bank{r}") for r in range(ROW_TILES)]
        mix(halves[1], [h_second[r][:] for r in range(ROW_TILES)])

        for r in range(ROW_TILES):
            last = r == ROW_TILES - 1
            members = ring.tile([P, H, MEMBERS], F32, name="members")
            denom = ring.tile([P, H], F32, name="denom")
            product = ring.tile([P, HALF], F32, name="product")
            shared = ring.tile([P, HALF], F32, name="shared")
            inverse = ring.tile([P, H], F32, name="inverse")
            result = ring.tile([P, H], F32, name="result")
            groups = member_groups(r)
            scale_after = {1, 2, len(groups) - 1} if last else {1, len(groups) - 1}
            fetched = 0
            scaled = 0
            for g, group in enumerate(groups):
                start = fetched
                for width in group:
                    fetch(
                        members[:, fetched : fetched + width, :].rearrange("p c m -> p (c m)"),
                        ex_rows[r],
                        n3_list,
                        MEMBERS * fetched,
                        MEMBERS * width,
                        scale=0.25,
                        bias=0.03125 * math.exp(SHIFT),
                    )
                    fetched = fetched + width
                couples = slice(start // 2, fetched // 2)
                nc.vector.tensor_reduce(denom[:, start:fetched], members[:, start:fetched, :], LAST_AXIS, ALU.add)
                nc.vector.tensor_reduce(
                    product[:, couples].rearrange("p (s c) -> p s c", c=MATE),
                    denom[:, start:fetched].rearrange("p (s h c) -> p s c h", h=2, c=MATE),
                    LAST_AXIS,
                    ALU.mult,
                )
                nc.vector.reciprocal(shared[:, couples], product[:, couples])
                if g in scale_after:
                    cols = slice(scaled, fetched)
                    engine = nc.vector if last and fetched == H else nc.gpsimd
                    common = shared[:, scaled // 2 : fetched // 2].rearrange("p (s c) -> p s c", c=MATE)
                    for h in range(2):
                        engine.tensor_tensor(
                            mates(inverse[:, cols])[:, :, h, :], common, mates(denom[:, cols])[:, :, 1 - h, :], ALU.mult
                        )
                    engine.tensor_tensor(result[:, cols], inverse[:, cols], ex_rows[r][:, cols], ALU.mult)
                    nc.sync.dma_start(out[r * P : (r + 1) * P, cols], result[:, cols])
                    scaled = fetched
